import numpy as np
import ml_dtypes


def mxq(x, axis, fmt="e4m3"):
    dtype, down = {"e4m3": (ml_dtypes.float8_e4m3fn, 7), "e5m2": (ml_dtypes.float8_e5m2, 14)}[fmt]
    v = np.moveaxis(np.asarray(x, np.float32).astype(ml_dtypes.bfloat16).astype(np.float64), axis, -1)
    blocks = v.reshape(v.shape[:-1] + (-1, 32))
    amax = np.abs(blocks).max(-1, keepdims=True)
    byte = np.maximum(np.where(amax > 0, np.frexp(amax)[1] - 1 + 127, 0) - down, 1)
    scale = np.exp2(byte - 127.0)
    codes = (blocks / scale).astype(np.float32).astype(dtype).astype(np.float64)
    return np.moveaxis((codes * scale).reshape(v.shape), -1, axis)


WIDE = False


def mx_kscale(k):
    if not WIDE:
        return np.ones(k)
    levels = np.array([10, -10, 5, -5, 0])
    if k % 512:
        return np.exp2(np.random.permutation(np.resize(levels, k // 32))).repeat(32)
    a = np.empty((k // 512, 16))
    for p in range(k // 512):
        a[p, :8] = np.random.permutation(np.resize(levels, 8))
        for g in range(8):
            far = levels[np.abs(levels - a[p, g]) >= 10]
            a[p, g + 8] = far[np.random.randint(len(far))]
    return np.exp2(a.ravel()).repeat(32)


def f64(x):
    return np.asarray(x).astype(np.float64)


def striped(idx):
    return np.tile(np.asarray(idx).reshape(-1, 16).T, (8, 1)).astype(np.uint16)


def unstriped(offs):
    return offs[:16].T.reshape(-1).astype(np.int64)


def bf(x):
    return np.asarray(x, np.float32).astype(ml_dtypes.bfloat16)


def planes(Y):
    r, m = Y.shape
    b = f64(bf(Y)).reshape(r // 32, 32, m)
    amax = np.abs(b).max(1)
    byte = np.clip(np.where(amax > 0, np.frexp(amax)[1] - 1 + 127 - 7, 1), 1, 254)
    codes = (b * np.exp2(127.0 - byte)[:, None, :]).reshape(r, m).astype(np.float32).astype(ml_dtypes.float8_e4m3fn).view(np.uint8)
    words = codes.reshape(r // 512, 128, 4, m).transpose(0, 1, 3, 2)
    return np.ascontiguousarray(words), np.ascontiguousarray(byte.astype(np.uint8).reshape(r // 512, 16, m))


D, T, I, Q, E, U = 512, 2048, 512, 256, 512, 1024


def setup_inputs():
    n = np.random.standard_normal
    idx = np.random.permutation(T)[:I]
    idx2 = np.random.permutation(U)[:I]
    fd = mx_kscale(D)
    fi = mx_kscale(I)
    ti = np.ones(T)
    ti[idx] = fi
    return {
        "query": (n((D, Q)) * 0.9 / np.sqrt(D) * fd[:, None]).astype(np.float32),
        "keys": (n((D, T)) / fd[:, None]).astype(np.float32),
        "notes": (n((D, U)) / fd[:, None]).astype(np.float32),
        "os": (np.random.uniform(0.02, 0.08, (1, I)) * fi).astype(np.float32),
        "vals": (n((E, T)) / ti).astype(np.float32),
        "offs": striped(idx),
        "offs2": striped(idx2),
    }


def reference(query, keys, notes, os, vals, offs, offs2):
    idx = unstriped(offs)
    idx2 = unstriped(offs2)
    zk = np.abs(f64(keys)[:, idx] - f64(notes)[:, idx2])
    queryq = mxq(f64(query), 0, "e4m3")
    zkq = mxq(zk, 0, "e4m3")
    s = queryq.T @ zkq
    w = np.maximum(s, 0.0)
    wo1 = w * f64(os)
    wt1 = wo1.T
    vt1 = f64(vals)[:, idx].T
    vt1q = mxq(vt1, 0, "e4m3")
    wt1q = mxq(wt1, 0, "e4m3")
    o = vt1q.T @ wt1q
    words, scales = planes(o)
    return o, words, scales

@@ -1,0 +1,196 @@
+from contextlib import ExitStack
+
+import concourse.mybir as mybir
+from concourse.masks import make_identity
+
+D, T, I, Q, E, U = 512, 2048, 512, 256, 512, 1024
+FLOPS = 2 * D * I * Q + 2 * I * E * Q
+
+F32 = mybir.dt.float32
+BF16 = mybir.dt.bfloat16
+I32 = mybir.dt.int32
+U32 = mybir.dt.uint32
+U16 = mybir.dt.uint16
+U8 = mybir.dt.uint8
+FP8X4 = mybir.dt.float8_e4m3fn_x4
+ALU = mybir.AluOpType
+ACT = mybir.ActivationFunctionType
+
+P = 128
+PACK = 4
+HALF = Q // 2
+LIST_COLS = I // 16
+VECTOR_COLS = 16
+
+
+def tile_attend_keyapart_read_lean_pl_kernel(tc, query, keys, notes, slot_factors, vals, offs, offs2, out_0, out_1, out_2):
+    nc = tc.nc
+    with ExitStack() as ctx:
+        held = ctx.enter_context(tc.tile_pool(name="held", bufs=1))
+        psum = ctx.enter_context(tc.psum_pool(name="psum", bufs=1))
+
+        def sb(name, shape, dtype, tag=None):
+            return held.tile(shape, dtype, name=name, tag=tag or name, align_bytes=64)
+
+        token_list = held.tile([P, LIST_COLS], U16, name="token_list")
+        note_list = held.tile([P, LIST_COLS], U16, name="note_list")
+        notes_sb = [sb(f"notes{t}", [P, U], F32) for t in range(PACK)]
+        keys_sb = [sb(f"keys{t}", [P, T], F32) for t in range(PACK)]
+        vals_sb = [sb(f"vals{t}", [P, T], F32) for t in range(PACK)]
+        query_sb = sb("query_sb", [P, PACK, Q], F32)
+        factor = sb("factor", [P, PACK], F32)
+
+        notes_rows = notes.rearrange("(p t) u -> p t u", t=PACK)
+        keys_rows = keys.rearrange("(p t) u -> p t u", t=PACK)
+        vals_rows = vals.rearrange("(p t) u -> p t u", t=PACK)
+        nc.sync.dma_start(notes_sb[0][:], notes_rows[:, 0, :])
+        nc.sync.dma_start(note_list[:], offs2)
+        nc.sync.dma_start(token_list[:], offs)
+        for t in range(1, PACK):
+            nc.sync.dma_start(notes_sb[t][:], notes_rows[:, t, :])
+        for t in range(PACK):
+            nc.sync.dma_start(keys_sb[t][:], keys_rows[:, t, :])
+        nc.sync.dma_start(query_sb[:], query.rearrange("(p t) q -> p t q", t=PACK))
+        nc.sync.dma_start(factor[:], slot_factors.rearrange("o (p r) -> (o p) r", r=PACK))
+        for t in range(PACK):
+            nc.sync.dma_start(vals_sb[t][:], vals_rows[:, t, :])
+
+        identity = sb("identity", [P, P], F32)
+        make_identity(nc, identity[:])
+
+        def quantize(codes, scales, src):
+            nc.vector.quantize_mx(out=codes.bitcast(FP8X4), scales=scales, in_=src)
+
+        picked_notes = [sb(f"picked_notes{t}", [P, I], F32) for t in range(PACK)]
+        for t in range(PACK):
+            nc.vector.tensor_copy(picked_notes[t][:], notes_sb[t][:].indirect(note_list[:]))
+
+        diffs = [sb(f"diff{u}", [P, 2, I], F32) for u in range(2)]
+        pairs = sb("pairs", [P, 2, 2 * I], BF16)
+        for u in range(2):
+            for e in range(2):
+                t = 2 * u + e
+                pieces = 2 if t == PACK - 1 else 1
+                for j in range(pieces):
+                    n = I // pieces
+                    slots = slice(j * n, (j + 1) * n)
+                    nc.vector.tensor_tensor(
+                        diffs[u][:, e, slots],
+                        keys_sb[t][:].indirect(token_list[:, j * n // 16 : (j + 1) * n // 16]),
+                        picked_notes[t][:, slots],
+                        ALU.subtract,
+                    )
+                    if e == 1:
+                        nc.scalar.activation(
+                            pairs[:, u, :].rearrange("p (r s e) -> p s r e", r=PACK, e=2)[:, j * n // PACK : (j + 1) * n // PACK],
+                            diffs[u][:, :, slots].rearrange("p e (s r) -> p s r e", r=PACK),
+                            ACT.Abs,
+                        )
+        query_bf = sb("query_bf", [P, Q, PACK], BF16)
+        query_codes = sb("query_codes", [P, Q], U32)
+        query_scales = sb("query_scales", [P, Q], U8)
+        nc.vector.tensor_copy(query_bf[:], query_sb[:].rearrange("p t q -> p q t"))
+        quantize(query_codes[:], query_scales[:], query_bf[:].rearrange("p q t -> p (q t)"))
+
+        zk_bf = [sb(f"zk_bf{j}", [P, I * PACK // 2], BF16) for j in range(2)]
+        zk_codes = sb("zk_codes", [P, I], U32)
+        zk_scales = sb("zk_scales", [P, I], U8)
+        pair_words = pairs[:].rearrange("p u x -> p (u x)").bitcast(F32).rearrange("p (u c) -> p c u", u=2)
+        for j in range(2):
+            cols = slice(j * I // 2, (j + 1) * I // 2)
+            nc.vector.tensor_copy(zk_bf[j][:].bitcast(F32).rearrange("p (c u) -> p c u", u=2), pair_words[:, cols, :])
+        for j in range(2):
+            cols = slice(j * I // 2, (j + 1) * I // 2)
+            quantize(zk_codes[:, cols], zk_scales[:, cols], zk_bf[j][:])
+
+        w_codes = sb("w_codes", [P, Q], U32)
+        w_scales = sb("w_scales", [P, Q], U8)
+        for h in range(2):
+            cols = slice(h * HALF, (h + 1) * HALF)
+            scores = psum.tile([P, PACK, HALF], F32, name=f"scores{h}")
+            for r in range(PACK):
+                slots = slice(r * P, (r + 1) * P)
+                nc.tensor.matmul_mx(
+                    out=scores[:, r, :],
+                    lhsT=zk_codes[:, slots].bitcast(FP8X4),
+                    lhsT_scale=zk_scales[:, slots],
+                    rhs=query_codes[:, cols].bitcast(FP8X4),
+                    rhs_scale=query_scales[:, cols],
+                    start=True,
+                    stop=True,
+                )
+            w_bf = sb(f"w_bf{h}", [P, HALF, PACK], BF16)
+            nc.vector.scalar_tensor_tensor(
+                w_bf[:],
+                scores[:].rearrange("p r q -> p q r"),
+                0.0,
+                factor[:].unsqueeze(1).to_broadcast([P, HALF, PACK]),
+                ALU.max,
+                ALU.mult,
+            )
+            quantize(w_codes[:, cols], w_scales[:, cols], w_bf[:].rearrange("p q r -> p (q r)"))
+
+        results = [psum.tile([P, PACK, HALF], F32, name=f"result{h}") for h in range(2)]
+        out_rows = out_0.rearrange("(p t) q -> p t q", t=PACK)
+
+        def store_rows(u):
+            rows = sb(f"rows{u}", [P, 2, Q], F32)
+            for h in (1, 0):
+                nc.scalar.copy(rows[:, :, h * HALF : (h + 1) * HALF], results[h][:, 2 * u : 2 * u + 2, :])
+            nc.sync.dma_start(out_rows[:, 2 * u : 2 * u + 2, :], rows[:])
+
+        def pick_and_turn(t):
+            picked = sb(f"picked_vals{t}", [P, I], BF16, tag={2: "w_bf1"}.get(t))
+            if t < 2:
+                nc.scalar.activation(picked[:], vals_sb[t][:].indirect(token_list[:]), ACT.Copy)
+            else:
+                cut = 16 * VECTOR_COLS
+                nc.vector.tensor_copy(picked[:, :cut], vals_sb[t][:].indirect(token_list[:, :VECTOR_COLS]))
+                nc.scalar.activation(picked[:, cut:], vals_sb[t][:].indirect(token_list[:, VECTOR_COLS:]), ACT.Copy)
+            words = picked[:].bitcast(F32)
+            turned = psum.tile([P, 2, P], F32, name=f"turned{t}")
+            for u in range(2):
+                nc.tensor.transpose(turned[:, u, :], words[:, u : 2 * P : 2], identity[:])
+            return turned
+
+        def multiply(t, turned):
+            v_bf = sb(f"v_bf{t}", [P, P * PACK], BF16, tag={0: "w_bf0", 2: "vals3"}.get(t))
+            (nc.vector.tensor_copy if t == 0 else nc.scalar.copy)(
+                v_bf[:].bitcast(F32).rearrange("p (e u) -> p e u", u=2),
+                turned[:].rearrange("p u e -> p e u"),
+            )
+            v_codes = sb(f"v_codes{t}", [P, P], U32)
+            v_scales = sb(f"v_scales{t}", [P, P], U8)
+            quantize(v_codes[:], v_scales[:], v_bf[:])
+            for h in range(2):
+                cols = slice(h * HALF, (h + 1) * HALF)
+                nc.tensor.matmul_mx(
+                    out=results[h][:, t, :],
+                    lhsT=v_codes[:].bitcast(FP8X4),
+                    lhsT_scale=v_scales[:],
+                    rhs=w_codes[:, cols].bitcast(FP8X4),
+                    rhs_scale=w_scales[:, cols],
+                    start=True,
+                    stop=True,
+                )
+
+        for t in range(2):
+            multiply(t, pick_and_turn(t))
+        store_rows(0)
+        last = [pick_and_turn(t) for t in (2, 3)]
+        for t in (2, 3):
+            multiply(t, last[t - 2])
+
+        out_codes = sb("out_codes", [P, Q], U32)
+        out_scales = sb("out_scales", [P, Q], U8)
+        out_bf = [sb(f"out_bf{h}", [P, HALF, PACK], BF16) for h in range(2)]
+        nc.vector.tensor_copy(out_bf[0][:], results[0][:].rearrange("p t q -> p q t"))
+        nc.scalar.copy(out_bf[1][:], results[1][:].rearrange("p t q -> p q t"))
+        for h in range(2):
+            cols = slice(h * HALF, (h + 1) * HALF)
+            quantize(out_codes[:, cols], out_scales[:, cols], out_bf[h][:].rearrange("p q t -> p (q t)"))
+        store_rows(1)
+        nc.sync.dma_start(out_1[0].rearrange("p c r -> p (c r)").bitcast(I32), out_codes[:].bitcast(I32))
+        for g in range(4):
+            queue = nc.sync if g < 2 else nc.scalar
+            queue.dma_start(out_2[0, 4 * g : 4 * g + 4, :].bitcast(I32), out_scales[32 * g : 32 * g + 4, :].bitcast(I32))

@@ -34,7 +34,7 @@ def tile_attend_keyapart_read_lean_pl_kernel(tc, query, keys, notes, slot_factor
 
         token_list = held.tile([P, LIST_COLS], U16, name="token_list")
         note_list = held.tile([P, LIST_COLS], U16, name="note_list")
-        notes_sb = [sb(f"notes{t}", [P, U], F32) for t in range(PACK)]
+        notes_sb = sb("notes_sb", [P, PACK, U], F32)
         keys_sb = [sb(f"keys{t}", [P, T], F32) for t in range(PACK)]
         vals_sb = [sb(f"vals{t}", [P, T], F32) for t in range(PACK)]
         query_sb = sb("query_sb", [P, PACK, Q], F32)
@@ -43,15 +43,13 @@ def tile_attend_keyapart_read_lean_pl_kernel(tc, query, keys, notes, slot_factor
         notes_rows = notes.rearrange("(p t) u -> p t u", t=PACK)
         keys_rows = keys.rearrange("(p t) u -> p t u", t=PACK)
         vals_rows = vals.rearrange("(p t) u -> p t u", t=PACK)
-        nc.sync.dma_start(notes_sb[0][:], notes_rows[:, 0, :])
+        nc.scalar.dma_start(notes_sb[:], notes_rows)
         nc.sync.dma_start(note_list[:], offs2)
         nc.sync.dma_start(token_list[:], offs)
-        for t in range(1, PACK):
-            nc.sync.dma_start(notes_sb[t][:], notes_rows[:, t, :])
+        nc.sync.dma_start(factor[:], slot_factors.rearrange("o (p r) -> (o p) r", r=PACK))
         for t in range(PACK):
             nc.sync.dma_start(keys_sb[t][:], keys_rows[:, t, :])
         nc.sync.dma_start(query_sb[:], query.rearrange("(p t) q -> p t q", t=PACK))
-        nc.sync.dma_start(factor[:], slot_factors.rearrange("o (p r) -> (o p) r", r=PACK))
         for t in range(PACK):
             nc.sync.dma_start(vals_sb[t][:], vals_rows[:, t, :])
 
@@ -63,7 +61,10 @@ def tile_attend_keyapart_read_lean_pl_kernel(tc, query, keys, notes, slot_factor
 
         picked_notes = [sb(f"picked_notes{t}", [P, I], F32) for t in range(PACK)]
         for t in range(PACK):
-            nc.vector.tensor_copy(picked_notes[t][:], notes_sb[t][:].indirect(note_list[:]))
+            if t % 2 == 0:
+                nc.vector.tensor_copy(picked_notes[t][:], notes_sb[:, t, :].indirect(note_list[:]))
+            else:
+                nc.scalar.activation(picked_notes[t][:], notes_sb[:, t, :].indirect(note_list[:]), ACT.Copy)
 
         diffs = [sb(f"diff{u}", [P, 2, I], F32) for u in range(2)]
         pairs = sb("pairs", [P, 2, 2 * I], BF16)
@@ -133,14 +134,8 @@ def tile_attend_keyapart_read_lean_pl_kernel(tc, query, keys, notes, slot_factor
         results = [psum.tile([P, PACK, HALF], F32, name=f"result{h}") for h in range(2)]
         out_rows = out_0.rearrange("(p t) q -> p t q", t=PACK)
 
-        def store_rows(u):
-            rows = sb(f"rows{u}", [P, 2, Q], F32)
-            for h in (1, 0):
-                nc.scalar.copy(rows[:, :, h * HALF : (h + 1) * HALF], results[h][:, 2 * u : 2 * u + 2, :])
-            nc.sync.dma_start(out_rows[:, 2 * u : 2 * u + 2, :], rows[:])
-
         def pick_and_turn(t):
-            picked = sb(f"picked_vals{t}", [P, I], BF16, tag={2: "w_bf1"}.get(t))
+            picked = sb(f"picked_vals{t}", [P, I], BF16, tag={2: "w_bf0"}.get(t))
             if t < 2:
                 nc.scalar.activation(picked[:], vals_sb[t][:].indirect(token_list[:]), ACT.Copy)
             else:
@@ -153,15 +148,14 @@ def tile_attend_keyapart_read_lean_pl_kernel(tc, query, keys, notes, slot_factor
                 nc.tensor.transpose(turned[:, u, :], words[:, u : 2 * P : 2], identity[:])
             return turned
 
-        def multiply(t, turned):
-            v_bf = sb(f"v_bf{t}", [P, P * PACK], BF16, tag={0: "w_bf0", 2: "vals3"}.get(t))
-            (nc.vector.tensor_copy if t == 0 else nc.scalar.copy)(
-                v_bf[:].bitcast(F32).rearrange("p (e u) -> p e u", u=2),
-                turned[:].rearrange("p u e -> p e u"),
-            )
-            v_codes = sb(f"v_codes{t}", [P, P], U32)
+        def quantize_turned(t, bank, copy, v_words, codes_tag=None):
+            copy(v_words.rearrange("p (e u) -> p e u", u=2), bank[:].rearrange("p u e -> p e u"))
+            v_codes = sb(f"v_codes{t}", [P, P], U32, tag=codes_tag)
             v_scales = sb(f"v_scales{t}", [P, P], U8)
-            quantize(v_codes[:], v_scales[:], v_bf[:])
+            quantize(v_codes[:], v_scales[:], v_words.bitcast(BF16))
+            return v_codes, v_scales
+
+        def multiply(t, v_codes, v_scales):
             for h in range(2):
                 cols = slice(h * HALF, (h + 1) * HALF)
                 nc.tensor.matmul_mx(
@@ -174,22 +168,35 @@ def tile_attend_keyapart_read_lean_pl_kernel(tc, query, keys, notes, slot_factor
                     stop=True,
                 )
 
-        for t in range(2):
-            multiply(t, pick_and_turn(t))
-        store_rows(0)
-        last = [pick_and_turn(t) for t in (2, 3)]
-        for t in (2, 3):
-            multiply(t, last[t - 2])
+        def copy_rows(rows, planes, copies, order):
+            for h in order:
+                copies[h](rows[:, :, h * HALF : (h + 1) * HALF], results[h][:, planes, :])
+
+        on_vector, on_scalar = nc.vector.tensor_copy, nc.scalar.copy
+        turned = [pick_and_turn(t) for t in range(2)]
+        v_words0 = sb("v_words0", [P, I // 2], F32, tag="w_bf0")
+        multiply(0, *quantize_turned(0, turned[0], on_vector, v_words0[:], codes_tag="picked_vals1"))
+        multiply(1, *quantize_turned(1, turned[1], on_scalar, sb("v_words1", [P, I // 2], F32)[:]))
+        turned += [pick_and_turn(t) for t in range(2, PACK)]
+        late = sb("late", [P, 3 * Q], F32, tag="vals3")
+        early_rows = late[:, : 2 * Q].rearrange("p (t q) -> p t q", q=Q)
+        operand2 = quantize_turned(2, turned[2], on_scalar, late[:, 2 * Q :])
+        copy_rows(early_rows, slice(0, 2), [on_vector, on_scalar], (0, 1))
+        nc.sync.dma_start(out_rows[:, 0:2, :], early_rows)
+        multiply(2, *operand2)
+        out_bf = sb("out_bf", [P, Q * PACK], BF16)
+        out_places = out_bf[:].rearrange("p (q t) -> p q t", t=PACK)
+        nc.vector.tensor_copy(out_places[:, :, 0:2], early_rows.rearrange("p t q -> p q t"))
+        multiply(3, *quantize_turned(3, turned[3], on_scalar, sb("v_words3", [P, I // 2], F32)[:]))
 
         out_codes = sb("out_codes", [P, Q], U32)
         out_scales = sb("out_scales", [P, Q], U8)
-        out_bf = [sb(f"out_bf{h}", [P, HALF, PACK], BF16) for h in range(2)]
-        nc.vector.tensor_copy(out_bf[0][:], results[0][:].rearrange("p t q -> p q t"))
-        nc.scalar.copy(out_bf[1][:], results[1][:].rearrange("p t q -> p q t"))
-        for h in range(2):
-            cols = slice(h * HALF, (h + 1) * HALF)
-            quantize(out_codes[:, cols], out_scales[:, cols], out_bf[h][:].rearrange("p q t -> p (q t)"))
-        store_rows(1)
+        last_rows = sb("last_rows", [P, 2, Q], F32)
+        for h, copy in enumerate((on_vector, on_scalar)):
+            copy(out_places[:, h * HALF : (h + 1) * HALF, 2:4], results[h][:, 2:4, :].rearrange("p t q -> p q t"))
+        copy_rows(last_rows[:], slice(2, 4), [on_vector, on_scalar], (0, 1))
+        nc.scalar.dma_start(out_rows[:, 2:4, :], last_rows[:])
+        quantize(out_codes[:], out_scales[:], out_bf[:])
         nc.sync.dma_start(out_1[0].rearrange("p c r -> p (c r)").bitcast(I32), out_codes[:].bitcast(I32))
         for g in range(4):
             queue = nc.sync if g < 2 else nc.scalar

@@ -27,6 +27,7 @@ def tile_attend_keyapart_read_lean_pl_kernel(tc, query, keys, notes, slot_factor
     nc = tc.nc
     with ExitStack() as ctx:
         held = ctx.enter_context(tc.tile_pool(name="held", bufs=1))
+        shared = ctx.enter_context(tc.tile_pool(name="shared", bufs=1))
         psum = ctx.enter_context(tc.psum_pool(name="psum", bufs=1))
 
         def sb(name, shape, dtype, tag=None):
@@ -36,7 +37,10 @@ def tile_attend_keyapart_read_lean_pl_kernel(tc, query, keys, notes, slot_factor
         note_list = held.tile([P, LIST_COLS], U16, name="note_list")
         notes_sb = sb("notes_sb", [P, PACK, U], F32)
         keys_sb = [sb(f"keys{t}", [P, T], F32) for t in range(PACK)]
-        vals_sb = [sb(f"vals{t}", [P, T], F32) for t in range(PACK)]
+        vals_sb = [
+            shared.tile([P, T], F32, name="vals2", align_bytes=64, offset=0) if t == 2 else sb(f"vals{t}", [P, T], F32)
+            for t in range(PACK)
+        ]
         query_sb = sb("query_sb", [P, PACK, Q], F32)
         factor = sb("factor", [P, PACK], F32)
 
@@ -87,11 +91,12 @@ def tile_attend_keyapart_read_lean_pl_kernel(tc, query, keys, notes, slot_factor
                             diffs[u][:, :, slots].rearrange("p e (s r) -> p s r e", r=PACK),
                             ACT.Abs,
                         )
-        query_bf = sb("query_bf", [P, Q, PACK], BF16)
+        query_bf = [sb(f"query_bf{h}", [P, HALF, PACK], BF16) for h in range(2)]
         query_codes = sb("query_codes", [P, Q], U32)
         query_scales = sb("query_scales", [P, Q], U8)
-        nc.vector.tensor_copy(query_bf[:], query_sb[:].rearrange("p t q -> p q t"))
-        quantize(query_codes[:], query_scales[:], query_bf[:].rearrange("p q t -> p (q t)"))
+        for h, copy in enumerate((nc.vector.tensor_copy, nc.scalar.copy)):
+            copy(query_bf[h][:], query_sb[:, :, h * HALF : (h + 1) * HALF].rearrange("p t q -> p q t"))
+        quantize(query_codes[:, :HALF], query_scales[:, :HALF], query_bf[0][:].rearrange("p q t -> p (q t)"))
 
         zk_bf = [sb(f"zk_bf{j}", [P, I * PACK // 2], BF16) for j in range(2)]
         zk_codes = sb("zk_codes", [P, I], U32)
@@ -103,6 +108,8 @@ def tile_attend_keyapart_read_lean_pl_kernel(tc, query, keys, notes, slot_factor
         for j in range(2):
             cols = slice(j * I // 2, (j + 1) * I // 2)
             quantize(zk_codes[:, cols], zk_scales[:, cols], zk_bf[j][:])
+
+        quantize(query_codes[:, HALF:], query_scales[:, HALF:], query_bf[1][:].rearrange("p q t -> p (q t)"))
 
         w_codes = sb("w_codes", [P, Q], U32)
         w_scales = sb("w_scales", [P, Q], U8)
@@ -135,7 +142,7 @@ def tile_attend_keyapart_read_lean_pl_kernel(tc, query, keys, notes, slot_factor
         out_rows = out_0.rearrange("(p t) q -> p t q", t=PACK)
 
         def pick_and_turn(t):
-            picked = sb(f"picked_vals{t}", [P, I], BF16, tag={2: "w_bf0"}.get(t))
+            picked = sb(f"picked_vals{t}", [P, I], BF16, tag={2: "w_bf1"}.get(t))
             if t < 2:
                 nc.scalar.activation(picked[:], vals_sb[t][:].indirect(token_list[:]), ACT.Copy)
             else:
@@ -148,9 +155,10 @@ def tile_attend_keyapart_read_lean_pl_kernel(tc, query, keys, notes, slot_factor
                 nc.tensor.transpose(turned[:, u, :], words[:, u : 2 * P : 2], identity[:])
             return turned
 
-        def quantize_turned(t, bank, copy, v_words, codes_tag=None):
+        def quantize_turned(t, bank, copy, v_words, v_codes=None):
             copy(v_words.rearrange("p (e u) -> p e u", u=2), bank[:].rearrange("p u e -> p e u"))
-            v_codes = sb(f"v_codes{t}", [P, P], U32, tag=codes_tag)
+            if v_codes is None:
+                v_codes = sb(f"v_codes{t}", [P, P], U32)
             v_scales = sb(f"v_scales{t}", [P, P], U8)
             quantize(v_codes[:], v_scales[:], v_words.bitcast(BF16))
             return v_codes, v_scales
@@ -173,11 +181,13 @@ def tile_attend_keyapart_read_lean_pl_kernel(tc, query, keys, notes, slot_factor
                 copies[h](rows[:, :, h * HALF : (h + 1) * HALF], results[h][:, planes, :])
 
         on_vector, on_scalar = nc.vector.tensor_copy, nc.scalar.copy
-        turned = [pick_and_turn(t) for t in range(2)]
-        v_words0 = sb("v_words0", [P, I // 2], F32, tag="w_bf0")
-        multiply(0, *quantize_turned(0, turned[0], on_vector, v_words0[:], codes_tag="picked_vals1"))
-        multiply(1, *quantize_turned(1, turned[1], on_scalar, sb("v_words1", [P, I // 2], F32)[:]))
-        turned += [pick_and_turn(t) for t in range(2, PACK)]
+        turned = [pick_and_turn(t) for t in range(3)]
+        v_codes0 = shared.tile([P, P], U32, name="v_codes0", align_bytes=64, offset=0)
+        v_words1 = shared.tile([P, I // 2], F32, name="v_words1", align_bytes=64, offset=4 * P)
+        v_words0 = sb("v_words0", [P, I // 2], F32, tag="vals1")
+        multiply(0, *quantize_turned(0, turned[0], on_scalar, v_words0[:], v_codes=v_codes0))
+        multiply(1, *quantize_turned(1, turned[1], on_scalar, v_words1[:]))
+        turned.append(pick_and_turn(3))
         late = sb("late", [P, 3 * Q], F32, tag="vals3")
         early_rows = late[:, : 2 * Q].rearrange("p (t q) -> p t q", q=Q)
         operand2 = quantize_turned(2, turned[2], on_scalar, late[:, 2 * Q :])

from contextlib import ExitStack

import concourse.mybir as mybir
from concourse.masks import make_identity

D, T, I, Q, E, U = 512, 2048, 512, 256, 512, 1024
FLOPS = 2 * D * I * Q + 2 * I * E * Q

F32 = mybir.dt.float32
BF16 = mybir.dt.bfloat16
I32 = mybir.dt.int32
U32 = mybir.dt.uint32
U16 = mybir.dt.uint16
U8 = mybir.dt.uint8
FP8X4 = mybir.dt.float8_e4m3fn_x4
ALU = mybir.AluOpType
ACT = mybir.ActivationFunctionType

P = 128
PACK = 4
HALF = Q // 2
LIST_COLS = I // 16
VECTOR_COLS = 16


def tile_attend_keyapart_read_lean_pl_kernel(tc, query, keys, notes, slot_factors, vals, offs, offs2, out_0, out_1, out_2):
    nc = tc.nc
    with ExitStack() as ctx:
        held = ctx.enter_context(tc.tile_pool(name="held", bufs=1))
        shared = ctx.enter_context(tc.tile_pool(name="shared", bufs=1))
        psum = ctx.enter_context(tc.psum_pool(name="psum", bufs=1))

        def sb(name, shape, dtype, tag=None):
            return held.tile(shape, dtype, name=name, tag=tag or name, align_bytes=64)

        token_list = held.tile([P, LIST_COLS], U16, name="token_list")
        note_list = held.tile([P, LIST_COLS], U16, name="note_list")
        notes_sb = sb("notes_sb", [P, PACK, U], F32)
        keys_sb = [sb(f"keys{t}", [P, T], F32) for t in range(PACK)]
        vals_sb = [
            shared.tile([P, T], F32, name="vals2", align_bytes=64, offset=0) if t == 2 else sb(f"vals{t}", [P, T], F32)
            for t in range(PACK)
        ]
        query_sb = sb("query_sb", [P, PACK, Q], F32)
        factor = sb("factor", [P, PACK], F32)

        notes_rows = notes.rearrange("(p t) u -> p t u", t=PACK)
        keys_rows = keys.rearrange("(p t) u -> p t u", t=PACK)
        vals_rows = vals.rearrange("(p t) u -> p t u", t=PACK)
        nc.scalar.dma_start(notes_sb[:], notes_rows)
        nc.sync.dma_start(note_list[:], offs2)
        nc.sync.dma_start(token_list[:], offs)
        nc.sync.dma_start(factor[:], slot_factors.rearrange("o (p r) -> (o p) r", r=PACK))
        for t in range(PACK):
            nc.sync.dma_start(keys_sb[t][:], keys_rows[:, t, :])
        nc.sync.dma_start(query_sb[:], query.rearrange("(p t) q -> p t q", t=PACK))
        for t in range(PACK):
            nc.sync.dma_start(vals_sb[t][:], vals_rows[:, t, :])

        identity = sb("identity", [P, P], F32)
        make_identity(nc, identity[:])

        def quantize(codes, scales, src):
            nc.vector.quantize_mx(out=codes.bitcast(FP8X4), scales=scales, in_=src)

        picked_notes = [sb(f"picked_notes{t}", [P, I], F32) for t in range(PACK)]
        for t in range(PACK):
            if t % 2 == 0:
                nc.vector.tensor_copy(picked_notes[t][:], notes_sb[:, t, :].indirect(note_list[:]))
            else:
                nc.scalar.activation(picked_notes[t][:], notes_sb[:, t, :].indirect(note_list[:]), ACT.Copy)

        diffs = [sb(f"diff{u}", [P, 2, I], F32) for u in range(2)]
        pairs = sb("pairs", [P, 2, 2 * I], BF16)
        for u in range(2):
            for e in range(2):
                t = 2 * u + e
                pieces = 2 if t == PACK - 1 else 1
                for j in range(pieces):
                    n = I // pieces
                    slots = slice(j * n, (j + 1) * n)
                    nc.vector.tensor_tensor(
                        diffs[u][:, e, slots],
                        keys_sb[t][:].indirect(token_list[:, j * n // 16 : (j + 1) * n // 16]),
                        picked_notes[t][:, slots],
                        ALU.subtract,
                    )
                    if e == 1:
                        nc.scalar.activation(
                            pairs[:, u, :].rearrange("p (r s e) -> p s r e", r=PACK, e=2)[:, j * n // PACK : (j + 1) * n // PACK],
                            diffs[u][:, :, slots].rearrange("p e (s r) -> p s r e", r=PACK),
                            ACT.Abs,
                        )
        query_bf = [sb(f"query_bf{h}", [P, HALF, PACK], BF16) for h in range(2)]
        query_codes = sb("query_codes", [P, Q], U32)
        query_scales = sb("query_scales", [P, Q], U8)
        for h, copy in enumerate((nc.vector.tensor_copy, nc.scalar.copy)):
            copy(query_bf[h][:], query_sb[:, :, h * HALF : (h + 1) * HALF].rearrange("p t q -> p q t"))
        quantize(query_codes[:, :HALF], query_scales[:, :HALF], query_bf[0][:].rearrange("p q t -> p (q t)"))

        zk_bf = [sb(f"zk_bf{j}", [P, I * PACK // 2], BF16) for j in range(2)]
        zk_codes = sb("zk_codes", [P, I], U32)
        zk_scales = sb("zk_scales", [P, I], U8)
        pair_words = pairs[:].rearrange("p u x -> p (u x)").bitcast(F32).rearrange("p (u c) -> p c u", u=2)
        for j in range(2):
            cols = slice(j * I // 2, (j + 1) * I // 2)
            nc.vector.tensor_copy(zk_bf[j][:].bitcast(F32).rearrange("p (c u) -> p c u", u=2), pair_words[:, cols, :])
        for j in range(2):
            cols = slice(j * I // 2, (j + 1) * I // 2)
            quantize(zk_codes[:, cols], zk_scales[:, cols], zk_bf[j][:])

        quantize(query_codes[:, HALF:], query_scales[:, HALF:], query_bf[1][:].rearrange("p q t -> p (q t)"))

        w_codes = sb("w_codes", [P, Q], U32)
        w_scales = sb("w_scales", [P, Q], U8)
        for h in range(2):
            cols = slice(h * HALF, (h + 1) * HALF)
            scores = psum.tile([P, PACK, HALF], F32, name=f"scores{h}")
            for r in range(PACK):
                slots = slice(r * P, (r + 1) * P)
                nc.tensor.matmul_mx(
                    out=scores[:, r, :],
                    lhsT=zk_codes[:, slots].bitcast(FP8X4),
                    lhsT_scale=zk_scales[:, slots],
                    rhs=query_codes[:, cols].bitcast(FP8X4),
                    rhs_scale=query_scales[:, cols],
                    start=True,
                    stop=True,
                )
            w_bf = sb(f"w_bf{h}", [P, HALF, PACK], BF16)
            nc.vector.scalar_tensor_tensor(
                w_bf[:],
                scores[:].rearrange("p r q -> p q r"),
                0.0,
                factor[:].unsqueeze(1).to_broadcast([P, HALF, PACK]),
                ALU.max,
                ALU.mult,
            )
            quantize(w_codes[:, cols], w_scales[:, cols], w_bf[:].rearrange("p q r -> p (q r)"))

        results = [psum.tile([P, PACK, HALF], F32, name=f"result{h}") for h in range(2)]
        out_rows = out_0.rearrange("(p t) q -> p t q", t=PACK)

        def pick_and_turn(t):
            picked = sb(f"picked_vals{t}", [P, I], BF16, tag={2: "w_bf1"}.get(t))
            if t < 2:
                nc.scalar.activation(picked[:], vals_sb[t][:].indirect(token_list[:]), ACT.Copy)
            else:
                cut = 16 * VECTOR_COLS
                nc.vector.tensor_copy(picked[:, :cut], vals_sb[t][:].indirect(token_list[:, :VECTOR_COLS]))
                nc.scalar.activation(picked[:, cut:], vals_sb[t][:].indirect(token_list[:, VECTOR_COLS:]), ACT.Copy)
            words = picked[:].bitcast(F32)
            turned = psum.tile([P, 2, P], F32, name=f"turned{t}")
            for u in range(2):
                nc.tensor.transpose(turned[:, u, :], words[:, u : 2 * P : 2], identity[:])
            return turned

        def quantize_turned(t, bank, copy, v_words, v_codes=None):
            copy(v_words.rearrange("p (e u) -> p e u", u=2), bank[:].rearrange("p u e -> p e u"))
            if v_codes is None:
                v_codes = sb(f"v_codes{t}", [P, P], U32)
            v_scales = sb(f"v_scales{t}", [P, P], U8)
            quantize(v_codes[:], v_scales[:], v_words.bitcast(BF16))
            return v_codes, v_scales

        def multiply(t, v_codes, v_scales):
            for h in range(2):
                cols = slice(h * HALF, (h + 1) * HALF)
                nc.tensor.matmul_mx(
                    out=results[h][:, t, :],
                    lhsT=v_codes[:].bitcast(FP8X4),
                    lhsT_scale=v_scales[:],
                    rhs=w_codes[:, cols].bitcast(FP8X4),
                    rhs_scale=w_scales[:, cols],
                    start=True,
                    stop=True,
                )

        def copy_rows(rows, planes, copies, order):
            for h in order:
                copies[h](rows[:, :, h * HALF : (h + 1) * HALF], results[h][:, planes, :])

        on_vector, on_scalar = nc.vector.tensor_copy, nc.scalar.copy
        turned = [pick_and_turn(t) for t in range(3)]
        v_codes0 = shared.tile([P, P], U32, name="v_codes0", align_bytes=64, offset=0)
        v_words1 = shared.tile([P, I // 2], F32, name="v_words1", align_bytes=64, offset=4 * P)
        v_words0 = sb("v_words0", [P, I // 2], F32, tag="vals1")
        multiply(0, *quantize_turned(0, turned[0], on_scalar, v_words0[:], v_codes=v_codes0))
        multiply(1, *quantize_turned(1, turned[1], on_scalar, v_words1[:]))
        turned.append(pick_and_turn(3))
        late = sb("late", [P, 3 * Q], F32, tag="vals3")
        early_rows = late[:, : 2 * Q].rearrange("p (t q) -> p t q", q=Q)
        operand2 = quantize_turned(2, turned[2], on_scalar, late[:, 2 * Q :])
        copy_rows(early_rows, slice(0, 2), [on_vector, on_scalar], (0, 1))
        nc.sync.dma_start(out_rows[:, 0:2, :], early_rows)
        multiply(2, *operand2)
        out_bf = sb("out_bf", [P, Q * PACK], BF16)
        out_places = out_bf[:].rearrange("p (q t) -> p q t", t=PACK)
        nc.vector.tensor_copy(out_places[:, :, 0:2], early_rows.rearrange("p t q -> p q t"))
        multiply(3, *quantize_turned(3, turned[3], on_scalar, sb("v_words3", [P, I // 2], F32)[:]))

        out_codes = sb("out_codes", [P, Q], U32)
        out_scales = sb("out_scales", [P, Q], U8)
        last_rows = sb("last_rows", [P, 2, Q], F32)
        for h, copy in enumerate((on_vector, on_scalar)):
            copy(out_places[:, h * HALF : (h + 1) * HALF, 2:4], results[h][:, 2:4, :].rearrange("p t q -> p q t"))
        copy_rows(last_rows[:], slice(2, 4), [on_vector, on_scalar], (0, 1))
        nc.scalar.dma_start(out_rows[:, 2:4, :], last_rows[:])
        quantize(out_codes[:], out_scales[:], out_bf[:])
        nc.sync.dma_start(out_1[0].rearrange("p c r -> p (c r)").bitcast(I32), out_codes[:].bitcast(I32))
        for g in range(4):
            queue = nc.sync if g < 2 else nc.scalar
            queue.dma_start(out_2[0, 4 * g : 4 * g + 4, :].bitcast(I32), out_scales[32 * g : 32 * g + 4, :].bitcast(I32))
